import numpy as np
import ml_dtypes


def mxq(x, axis, fmt="e4m3"):
    dtype, down = {"e4m3": (ml_dtypes.float8_e4m3fn, 7), "e5m2": (ml_dtypes.float8_e5m2, 14)}[fmt]
    v = np.moveaxis(np.asarray(x, np.float32).astype(ml_dtypes.bfloat16).astype(np.float64), axis, -1)
    blocks = v.reshape(v.shape[:-1] + (-1, 32))
    amax = np.abs(blocks).max(-1, keepdims=True)
    byte = np.maximum(np.where(amax > 0, np.frexp(amax)[1] - 1 + 127, 0) - down, 1)
    scale = np.exp2(byte - 127.0)
    codes = (blocks / scale).astype(np.float32).astype(dtype).astype(np.float64)
    return np.moveaxis((codes * scale).reshape(v.shape), -1, axis)


WIDE = False


def mx_kscale(k):
    if not WIDE:
        return np.ones(k)
    levels = np.array([10, -10, 5, -5, 0])
    if k % 512:
        return np.exp2(np.random.permutation(np.resize(levels, k // 32))).repeat(32)
    a = np.empty((k // 512, 16))
    for p in range(k // 512):
        a[p, :8] = np.random.permutation(np.resize(levels, 8))
        for g in range(8):
            far = levels[np.abs(levels - a[p, g]) >= 10]
            a[p, g + 8] = far[np.random.randint(len(far))]
    return np.exp2(a.ravel()).repeat(32)


def f64(x):
    return np.asarray(x).astype(np.float64)


def striped(idx):
    return np.tile(idx.reshape(-1, 16).T, (8, 1)).astype(np.uint16)


def unstriped(offs):
    return offs[:16].T.reshape(-1).astype(np.int64)


def sigmoid(v):
    return 1.0 / (1.0 + np.exp(-np.maximum(v, -700.0)))


K, T, E, C, H, N = 512, 1536, 4, 256, 512, 128


def by_expert(wq, xq):
    return np.concatenate([wq[e].T @ xq[:, e * C:(e + 1) * C] for e in range(E)], axis=1)


def setup_inputs():
    n = np.random.standard_normal
    s = mx_kscale(K)[:, None]
    u = mx_kscale(H)
    return {
        "xT": (n((K, T)) * s).astype(np.float32),
        "w1": (n((E, K, H)) / np.sqrt(K) / s[None]).astype(np.float32),
        "w3": (n((E, K, H)) / np.sqrt(K) / s[None] * u[None, None, :]).astype(np.float32),
        "w2": (n((E, H, N)) / np.sqrt(H) / u[None, :, None]).astype(np.float32),
        "gate": np.tile(np.random.uniform(0.2, 1.0, E * C), (N, 1)).astype(np.float32),
        "offs": striped(np.random.permutation(T)[:E * C]),
    }


def reference(xT, w1, w3, w2, gate, offs):
    idx = unstriped(offs)
    xq = mxq(f64(xT)[:, idx], 0, "e4m3")
    h = sigmoid(by_expert(mxq(f64(w1), 1, "e4m3"), xq))
    h = h * by_expert(mxq(f64(w3), 1, "e4m3"), xq)
    y = by_expert(mxq(f64(w2), 1, "e4m3"), mxq(h, 0, "e4m3"))
    out = np.zeros((N, T))
    out[:, idx] = f64(gate) * y
    return out

@@ -1,0 +1,307 @@
+from contextlib import ExitStack
+
+import concourse.mybir as mybir
+
+K, T, E, C, H, N = 512, 1536, 4, 256, 512, 128
+P = 128
+J = 4
+SLOTS = E * C
+FLOPS = 2 * SLOTS * (2 * K * H + H * N)
+
+F32 = mybir.dt.float32
+BF16 = mybir.dt.bfloat16
+U32 = mybir.dt.uint32
+U16 = mybir.dt.uint16
+U8 = mybir.dt.uint8
+FP8X4 = mybir.dt.float8_e4m3fn_x4
+MULT = mybir.AluOpType.mult
+ADD = mybir.AluOpType.add
+SIGMOID = mybir.ActivationFunctionType.Sigmoid
+
+HALF = 128
+SCATTER = 'd'
+XS = [512, 512, 256, 256]
+LOADS = ['offs', 'x0', 'x1', 'x2', 'x3', 'w2r1', 'w1r0', 'w3r0', 'w1r1', 'w2r0', 'w3r1', 'w1r2', 'w2r3', 'w3r2', 'gate', 'w1r3', 'w3r3', 'w2r2']
+ORDER = [
+    ('wi', 'w1', 3, 'S', 0, 128),
+    ('wi', 'w3', 0, 'S', 8, 128),
+    ('wi', 'w1', 2, 'S', 16, 128),
+    ('xi', 0, 'S', 384, 512),
+    ('xi', 1, 'S', 384, 512),
+    ('xi', 2, 'S', 128, 256),
+    ('xi', 3, 'S', 192, 256),
+    ('xi', 0, 'V', 0, 384),
+    ('xq', 0),
+    ('xi', 1, 'V', 0, 384),
+    ('xq', 1),
+    ('xi', 2, 'V', 0, 128),
+    ('xq', 2),
+    ('xi', 3, 'V', 0, 192),
+    ('xq', 3),
+    ('g', 'b', 0, 512),
+    ('wi', 'w1', 2, 'V', 0, 16),
+    ('wi', 'w2', 0, 'V', 0, 128),
+    ('wi', 'w3', 1, 'S', 104, 128),
+    ('wi', 'w2', 3, 'S', 0, 128),
+    ('wq', 'w2', 3),
+    ('wq', 'w2', 0),
+    ('wi', 'w3', 0, 'V', 0, 8),
+    ('wq', 'w3', 0),
+    ('wi', 'w1', 1, 'V', 0, 80),
+    ('wq', 'w1', 2),
+    ('wi', 'w3', 3, 'V', 0, 16),
+    ('wi', 'w3', 2, 'V', 0, 128),
+    ('wq', 'w3', 2),
+    ('g', 'w', 512, 1024),
+    ('wi', 'w2', 1, 'S', 0, 128),
+    ('wi', 'w1', 0, 'S', 0, 128),
+    ('wi', 'w1', 1, 'S', 80, 128),
+    ('wq', 'w1', 1),
+    ('wq', 'w2', 1),
+    ('wi', 'w3', 1, 'V', 0, 104),
+    ('wq', 'w3', 1),
+    ('g', 'b', 512, 1024),
+    ('wq', 'w1', 0),
+    ('wi', 'w3', 3, 'S', 16, 128),
+    ('wq', 'w3', 3),
+    ('wi', 'w2', 2, 'S', 0, 128),
+    ('wq', 'w2', 2),
+    ('g', 'w', 0, 512),
+    ('first', 'b', 0, 0),
+    ('first', 'a', 1, 0),
+    ('sig', 1, 0),
+    ('first', 'a', 2, 1),
+    ('sig', 2, 1),
+    ('first', 'a', 0, 0),
+    ('sig', 0, 0),
+    ('first', 'a', 1, 1),
+    ('sig', 1, 1),
+    ('first', 'a', 0, 1),
+    ('h', 0, 0),
+    ('first', 'b', 1, 1),
+    ('h', 1, 1),
+    ('first', 'b', 3, 0),
+    ('sig', 0, 1),
+    ('first', 'a', 2, 0),
+    ('sig', 2, 0),
+    ('wq', 'w1', 3),
+    ('first', 'a', 3, 0),
+    ('first', 'a', 3, 1),
+    ('sig', 3, 0),
+    ('sig', 3, 1),
+    ('h', 3, 0),
+    ('first', 'b', 1, 0),
+    ('h', 1, 0),
+    ('hq', 1),
+    ('first', 'b', 2, 1),
+    ('h', 2, 1),
+    ('y', 1),
+    ('yc', 1),
+    ('first', 'b', 0, 1),
+    ('h', 0, 1),
+    ('first', 'b', 2, 0),
+    ('h', 2, 0),
+    ('hq', 2),
+    ('hq', 0),
+    ('first', 'b', 3, 1),
+    ('h', 3, 1),
+    ('hq', 3),
+    ('y', 3),
+    ('yc', 3),
+    ('y', 0),
+    ('yc', 0),
+    ('scat', 0),
+    ('y', 2),
+    ('scat', 1),
+    ('yc', 2),
+    ('scat', 2),
+    ('scat', 3),
+]
+
+
+def tile_routed_moe_kernel(tc, xT, w1, w3, w2, gate, offs, out):
+    nc = tc.nc
+    with ExitStack() as ctx:
+        held = ctx.enter_context(tc.tile_pool(name="held", bufs=1))
+        ring = ctx.enter_context(tc.tile_pool(name="ring", bufs=3))
+        psum = ctx.enter_context(tc.psum_pool(name="psum", bufs=3))
+        psum_y = ctx.enter_context(tc.psum_pool(name="psum_y", bufs=2))
+
+        offsets = held.tile([P, SLOTS // 16], U16, name="offsets")
+        x_view = xT.rearrange("(p j) n -> p j n", j=J)
+        gate_sb = held.tile([P, SLOTS], F32, name="gate_sb")
+        x_words = held.tile([P, T], U32, name="x_words", align_bytes=64)
+        x_bytes = held.tile([P, T], U8, name="x_bytes", align_bytes=64)
+        window = held.tile([P, T], F32, name="window", align_bytes=64)
+        g_words = held.tile([P, SLOTS], U32, name="g_words", align_bytes=64)
+        g_bytes = held.tile([P, SLOTS], U8, name="g_bytes", align_bytes=64)
+        d = {}
+        WEIGHTS = {"w1": (w1, H), "w3": (w3, H), "w2": (w2, N)}
+
+        def load(name):
+            if name == "offs":
+                nc.sync.dma_start(offsets[:], offs)
+            elif name == "gate":
+                nc.sync.dma_start(gate_sb[:], gate)
+            elif name.startswith("x"):
+                s = int(name[1:])
+                lo = sum(XS[:s])
+                t = held.tile([P, J, XS[s]], F32, name=f"{name}_raw", align_bytes=64)
+                nc.sync.dma_start(t[:], x_view[:, :, lo : lo + XS[s]])
+                d[name] = t
+            else:
+                src, width = WEIGHTS[name[0:2]]
+                t = held.tile([P, J, width], F32, name=f"{name}_raw", align_bytes=64)
+                nc.sync.dma_start(t[:], src[int(name[3:])].rearrange("(p j) n -> p j n", j=J))
+                d[name] = t
+
+        for name in LOADS:
+            load(name)
+
+        warm = held.tile([P, 1], F32, name="warm")
+        nc.vector.memset(warm[:], 0.0)
+        warm_out = held.tile([P, 1], F32, name="warm_out")
+        nc.scalar.activation(warm_out[:], warm[:], SIGMOID)
+        nc.gpsimd.memset(x_bytes[:], 0)
+        nc.vector.memset(window[:], 0.0)
+
+        def gp_copy(out, in_):
+            nc.gpsimd.tensor_scalar(out, in_, 1.0, 0.0, MULT, ADD)
+
+        COPY = {"V": nc.vector.tensor_copy, "S": nc.scalar.copy, "G": gp_copy, "P": nc.gpsimd.tensor_copy}
+
+        def grouped(name, width):
+            if name not in d:
+                g = held.tile([P, width, J], BF16, name=f"{name}_g", align_bytes=64)
+                d[name] = g
+            return d[name]
+
+        def plain(eng, g, raw, lo, hi):
+            COPY[eng](
+                g[:, lo:hi, :].rearrange("p (c i) j -> p c j i", i=4),
+                raw[:, :, lo:hi].rearrange("p j (c i) -> p c j i", i=4),
+            )
+
+        def permuted(eng, g, raw, lo, hi):
+            COPY[eng](
+                g[:].rearrange("p (t m) j -> p m j t", t=J)[:, lo:hi],
+                raw[:].rearrange("p j (m t) -> p m j t", t=J)[:, lo:hi],
+            )
+
+        def flat(g):
+            return g[:].rearrange("p n j -> p (n j)")
+
+        def x_il(s, eng, lo, hi):
+            plain(eng, grouped(f"xg{s}", XS[s]), d[f"x{s}"], lo, hi)
+
+        def x_q(s):
+            lo = sum(XS[:s])
+            cols = slice(lo, lo + XS[s])
+            nc.vector.quantize_mx(out=x_words[:, cols].bitcast(FP8X4), scales=x_bytes[:, cols], in_=flat(d[f"xg{s}"]))
+
+        def gather(kind, lo, hi):
+            o = offsets[:, lo // 16 : hi // 16]
+            if kind == "w":
+                nc.vector.tensor_copy(g_words[:, lo:hi], x_words[:].indirect(o))
+            else:
+                nc.vector.tensor_copy(g_bytes[:, lo:hi], x_bytes[:].indirect(o))
+
+        def w_il(w, e, eng, lo, hi):
+            if w == "w2":
+                plain(eng, grouped(f"w2g{e}", N), d[f"w2r{e}"], lo, hi)
+            else:
+                permuted(eng, grouped(f"{w}g{e}", H), d[f"{w}r{e}"], lo, hi)
+
+        def quantise(name, g, width):
+            words = held.tile([P, width], U32, name=f"{name}_words", align_bytes=64)
+            scales = held.tile([P, width], U8, name=f"{name}_bytes", align_bytes=64)
+            nc.vector.quantize_mx(out=words[:].bitcast(FP8X4), scales=scales[:], in_=flat(g))
+            d[name] = (words, scales)
+
+        def first(k, e, hf):
+            wq = d[("w1" if k == "a" else "w3") + f"q{e}"]
+            bank = psum.tile([P, J, HALF], F32, name=k)
+            cols = slice(e * C + hf * HALF, e * C + (hf + 1) * HALF)
+            for t in range(J):
+                m = slice(t * P, (t + 1) * P)
+                nc.tensor.matmul_mx(
+                    out=bank[:, t, :],
+                    lhsT=wq[0][:, m].bitcast(FP8X4),
+                    lhsT_scale=wq[1][:, m],
+                    rhs=g_words[:, cols].bitcast(FP8X4),
+                    rhs_scale=g_bytes[:, cols],
+                    start=True,
+                    stop=True,
+                )
+            d[f"{k}{e}{hf}"] = bank
+
+        def sig(e, hf):
+            sg = held.tile([P, HALF, J], F32, name=f"sig{e}{hf}")
+            nc.scalar.activation(sg[:], d[f"a{e}{hf}"][:].rearrange("p t c -> p c t"), SIGMOID)
+            d[f"sig{e}{hf}"] = sg
+
+        def hidden(e, hf):
+            h = grouped(f"h{e}", C)
+            nc.vector.tensor_tensor(
+                h[:, hf * HALF : (hf + 1) * HALF, :],
+                d[f"sig{e}{hf}"][:],
+                d[f"b{e}{hf}"][:].rearrange("p t c -> p c t"),
+                MULT,
+            )
+
+        def second(e):
+            y = psum_y.tile([P, C], F32, name="y")
+            hq, w2q = d[f"hq{e}"], d[f"w2q{e}"]
+            nc.tensor.matmul_mx(
+                out=y[:],
+                lhsT=w2q[0][:].bitcast(FP8X4),
+                lhsT_scale=w2q[1][:],
+                rhs=hq[0][:].bitcast(FP8X4),
+                rhs_scale=hq[1][:],
+                start=True,
+                stop=True,
+            )
+            d[f"y{e}"] = y
+
+        def y_copy(e):
+            t = held.tile([P, C], F32, name=f"yc{e}")
+            if SCATTER == "d":
+                nc.scalar.copy(t[:], d[f"y{e}"][:])
+            else:
+                nc.vector.tensor_tensor(t[:], d[f"y{e}"][:], gate_sb[:, e * C : (e + 1) * C], MULT)
+            d[f"yc{e}"] = t
+
+        def scatter(e):
+            w = window[:].indirect(offsets[:, e * (C // 16) : (e + 1) * (C // 16)])
+            if SCATTER == "d":
+                nc.vector.tensor_tensor(w, d[f"yc{e}"][:], gate_sb[:, e * C : (e + 1) * C], MULT)
+            else:
+                nc.vector.tensor_copy(w, d[f"yc{e}"][:])
+
+        for o in ORDER:
+            k = o[0]
+            if k == "xi":
+                x_il(o[1], o[2], o[3], o[4])
+            elif k == "xq":
+                x_q(o[1])
+            elif k == "g":
+                gather(o[1], o[2], o[3])
+            elif k == "wi":
+                w_il(o[1], o[2], o[3], o[4], o[5])
+            elif k == "wq":
+                quantise(f"{o[1]}q{o[2]}", d[f"{o[1]}g{o[2]}"], N if o[1] == "w2" else H)
+            elif k == "hq":
+                quantise(f"hq{o[1]}", d[f"h{o[1]}"], C)
+            elif k == "first":
+                first(o[1], o[2], o[3])
+            elif k == "sig":
+                sig(o[1], o[2])
+            elif k == "h":
+                hidden(o[1], o[2])
+            elif k == "y":
+                second(o[1])
+            elif k == "yc":
+                y_copy(o[1])
+            else:
+                scatter(o[1])
+        nc.sync.dma_start(out, window[:])

@@ -20,101 +20,98 @@ SIGMOID = mybir.ActivationFunctionType.Sigmoid
 
 HALF = 128
 SCATTER = 'd'
-XS = [512, 512, 256, 256]
-LOADS = ['offs', 'x0', 'x1', 'x2', 'x3', 'w2r1', 'w1r0', 'w3r0', 'w1r1', 'w2r0', 'w3r1', 'w1r2', 'w2r3', 'w3r2', 'gate', 'w1r3', 'w3r3', 'w2r2']
+XPC = [(0, 0, 768), (0, 768, 1536), (1, 0, 896), (1, 896, 1536)]
+XQ = [0, 512]
+LOADS = ['x0', 'x1', 'offs', 'x2', 'x3', 'w1r0', 'w3r0', 'w1r1', 'w3r1', 'w2r0', 'w1r2', 'w1r3', 'w3r2', 'gate0', 'w3r3', 'w2r1', 'gate1']
 ORDER = [
-    ('wi', 'w1', 3, 'S', 0, 128),
-    ('wi', 'w3', 0, 'S', 8, 128),
-    ('wi', 'w1', 2, 'S', 16, 128),
-    ('xi', 0, 'S', 384, 512),
-    ('xi', 1, 'S', 384, 512),
-    ('xi', 2, 'S', 128, 256),
-    ('xi', 3, 'S', 192, 256),
-    ('xi', 0, 'V', 0, 384),
-    ('xq', 0),
-    ('xi', 1, 'V', 0, 384),
-    ('xq', 1),
+    ('xi', 0, 'V', 0, 448),
+    ('xi', 0, 'S', 448, 768),
+    ('xi', 1, 'S', 576, 768),
+    ('xi', 1, 'V', 0, 576),
+    ('g', 0, 0, 1024),
+    ('xi', 2, 'S', 128, 896),
     ('xi', 2, 'V', 0, 128),
-    ('xq', 2),
-    ('xi', 3, 'V', 0, 192),
-    ('xq', 3),
-    ('g', 'b', 0, 512),
-    ('wi', 'w1', 2, 'V', 0, 16),
-    ('wi', 'w2', 0, 'V', 0, 128),
-    ('wi', 'w3', 1, 'S', 104, 128),
-    ('wi', 'w2', 3, 'S', 0, 128),
-    ('wq', 'w2', 3),
-    ('wq', 'w2', 0),
-    ('wi', 'w3', 0, 'V', 0, 8),
-    ('wq', 'w3', 0),
-    ('wi', 'w1', 1, 'V', 0, 80),
-    ('wq', 'w1', 2),
-    ('wi', 'w3', 3, 'V', 0, 16),
-    ('wi', 'w3', 2, 'V', 0, 128),
-    ('wq', 'w3', 2),
-    ('g', 'w', 512, 1024),
-    ('wi', 'w2', 1, 'S', 0, 128),
+    ('xi', 3, 'V', 0, 512),
+    ('xi', 3, 'S', 512, 640),
+    ('g', 1, 0, 512),
     ('wi', 'w1', 0, 'S', 0, 128),
-    ('wi', 'w1', 1, 'S', 80, 128),
-    ('wq', 'w1', 1),
-    ('wq', 'w2', 1),
-    ('wi', 'w3', 1, 'V', 0, 104),
-    ('wq', 'w3', 1),
-    ('g', 'b', 512, 1024),
+    ('g', 1, 512, 1024),
+    ('xq', 0, 512),
+    ('xq', 512, 1024),
+    ('wi', 'w3', 0, 'S', 32, 128),
     ('wq', 'w1', 0),
-    ('wi', 'w3', 3, 'S', 16, 128),
-    ('wq', 'w3', 3),
-    ('wi', 'w2', 2, 'S', 0, 128),
-    ('wq', 'w2', 2),
-    ('g', 'w', 0, 512),
-    ('first', 'b', 0, 0),
-    ('first', 'a', 1, 0),
-    ('sig', 1, 0),
-    ('first', 'a', 2, 1),
-    ('sig', 2, 1),
+    ('wi', 'w3', 0, 'V', 0, 32),
     ('first', 'a', 0, 0),
-    ('sig', 0, 0),
-    ('first', 'a', 1, 1),
-    ('sig', 1, 1),
+    ('wi', 'w1', 1, 'S', 96, 128),
+    ('wi', 'w1', 1, 'V', 0, 96),
     ('first', 'a', 0, 1),
-    ('h', 0, 0),
-    ('first', 'b', 1, 1),
-    ('h', 1, 1),
-    ('first', 'b', 3, 0),
+    ('sig', 0, 0),
+    ('wq', 'w3', 0),
     ('sig', 0, 1),
-    ('first', 'a', 2, 0),
-    ('sig', 2, 0),
-    ('wq', 'w1', 3),
-    ('first', 'a', 3, 0),
-    ('first', 'a', 3, 1),
-    ('sig', 3, 0),
-    ('sig', 3, 1),
-    ('h', 3, 0),
-    ('first', 'b', 1, 0),
-    ('h', 1, 0),
-    ('hq', 1),
-    ('first', 'b', 2, 1),
-    ('h', 2, 1),
-    ('y', 1),
-    ('yc', 1),
+    ('wq', 'w1', 1),
+    ('first', 'b', 0, 0),
     ('first', 'b', 0, 1),
+    ('wi', 'w3', 1, 'V', 0, 56),
+    ('wi', 'w3', 1, 'S', 56, 128),
+    ('first', 'a', 1, 0),
+    ('h', 0, 0),
+    ('first', 'a', 1, 1),
     ('h', 0, 1),
-    ('first', 'b', 2, 0),
-    ('h', 2, 0),
-    ('hq', 2),
+    ('wi', 'w2', 0, 'S', 0, 128),
+    ('wq', 'w3', 1),
     ('hq', 0),
+    ('first', 'b', 1, 0),
+    ('sig', 1, 0),
+    ('wi', 'w1', 2, 'V', 0, 64),
+    ('first', 'b', 1, 1),
+    ('sig', 1, 1),
+    ('wq', 'w2', 0),
+    ('h', 1, 0),
+    ('y', 0),
+    ('wi', 'w1', 2, 'S', 64, 128),
+    ('h', 1, 1),
+    ('wi', 'w1', 3, 'V', 0, 64),
+    ('wi', 'w1', 3, 'S', 64, 128),
+    ('hq', 1),
+    ('wq', 'w1', 2),
+    ('y', 1),
+    ('yc', 0),
+    ('wq', 'w1', 3),
+    ('first', 'a', 2, 0),
+    ('wi', 'w3', 2, 'S', 40, 128),
+    ('first', 'a', 2, 1),
+    ('wi', 'w3', 2, 'V', 0, 40),
+    ('first', 'a', 3, 0),
+    ('scat', 0),
+    ('yc', 1),
+    ('sig', 2, 0),
+    ('wq', 'w3', 2),
+    ('wi', 'w3', 3, 'S', 40, 128),
+    ('first', 'a', 3, 1),
+    ('wi', 'w3', 3, 'V', 0, 40),
+    ('first', 'b', 2, 0),
+    ('scat', 1),
+    ('first', 'b', 2, 1),
+    ('wi', 'w2', 1, 'S', 0, 128),
+    ('wq', 'w3', 3),
+    ('sig', 2, 1),
+    ('h', 2, 0),
+    ('first', 'b', 3, 0),
+    ('wq', 'w2', 1),
+    ('sig', 3, 1),
     ('first', 'b', 3, 1),
+    ('h', 2, 1),
+    ('sig', 3, 0),
     ('h', 3, 1),
-    ('hq', 3),
+    ('hq', 2),
+    ('h', 3, 0),
+    ('y', 2),
+    ('yc', 2),
+    ('hqh', 3, 1),
+    ('hqh', 3, 0),
+    ('scat', 2),
     ('y', 3),
     ('yc', 3),
-    ('y', 0),
-    ('yc', 0),
-    ('scat', 0),
-    ('y', 2),
-    ('scat', 1),
-    ('yc', 2),
-    ('scat', 2),
     ('scat', 3),
 ]
 
@@ -123,31 +120,33 @@ def tile_routed_moe_kernel(tc, xT, w1, w3, w2, gate, offs, out):
     nc = tc.nc
     with ExitStack() as ctx:
         held = ctx.enter_context(tc.tile_pool(name="held", bufs=1))
-        ring = ctx.enter_context(tc.tile_pool(name="ring", bufs=3))
         psum = ctx.enter_context(tc.psum_pool(name="psum", bufs=3))
         psum_y = ctx.enter_context(tc.psum_pool(name="psum_y", bufs=2))
 
         offsets = held.tile([P, SLOTS // 16], U16, name="offsets")
-        x_view = xT.rearrange("(p j) n -> p j n", j=J)
+        x_view = xT.rearrange("(p u e) n -> u p e n", u=2, e=2)
         gate_sb = held.tile([P, SLOTS], F32, name="gate_sb")
-        x_words = held.tile([P, T], U32, name="x_words", align_bytes=64)
-        x_bytes = held.tile([P, T], U8, name="x_bytes", align_bytes=64)
+        x_pairs = [held.tile([P, T, 2], BF16, name=f"x_pairs{u}", align_bytes=64) for u in range(2)]
+        g_x = held.tile([P, SLOTS, J], BF16, name="g_x", align_bytes=64)
         window = held.tile([P, T], F32, name="window", align_bytes=64)
-        g_words = held.tile([P, SLOTS], U32, name="g_words", align_bytes=64)
-        g_bytes = held.tile([P, SLOTS], U8, name="g_bytes", align_bytes=64)
         d = {}
-        WEIGHTS = {"w1": (w1, H), "w3": (w3, H), "w2": (w2, N)}
+        WEIGHTS = {"w1": (w1, H), "w3": (w3, H)}
 
         def load(name):
             if name == "offs":
                 nc.sync.dma_start(offsets[:], offs)
-            elif name == "gate":
-                nc.sync.dma_start(gate_sb[:], gate)
+            elif name.startswith("gate"):
+                cols = slice(int(name[4:]) * 2 * C, (int(name[4:]) + 1) * 2 * C)
+                nc.sync.dma_start(gate_sb[:, cols], gate[:, cols])
             elif name.startswith("x"):
-                s = int(name[1:])
-                lo = sum(XS[:s])
-                t = held.tile([P, J, XS[s]], F32, name=f"{name}_raw", align_bytes=64)
-                nc.sync.dma_start(t[:], x_view[:, :, lo : lo + XS[s]])
+                u, lo, hi = XPC[int(name[1:])]
+                t = held.tile([P, 2, hi - lo], F32, name=f"{name}_raw", align_bytes=64)
+                nc.sync.dma_start(t[:], x_view[u][:, :, lo:hi])
+                d[name] = t
+            elif name.startswith("w2"):
+                k = int(name[3:])
+                t = held.tile([P, 2, J, N], F32, name=f"{name}_raw", align_bytes=64)
+                nc.sync.dma_start(t[:], w2[2 * k : 2 * k + 2].rearrange("e (p j) n -> p e j n", j=J))
                 d[name] = t
             else:
                 src, width = WEIGHTS[name[0:2]]
@@ -162,7 +161,6 @@ def tile_routed_moe_kernel(tc, xT, w1, w3, w2, gate, offs, out):
         nc.vector.memset(warm[:], 0.0)
         warm_out = held.tile([P, 1], F32, name="warm_out")
         nc.scalar.activation(warm_out[:], warm[:], SIGMOID)
-        nc.gpsimd.memset(x_bytes[:], 0)
         nc.vector.memset(window[:], 0.0)
 
         def gp_copy(out, in_):
@@ -176,12 +174,6 @@ def tile_routed_moe_kernel(tc, xT, w1, w3, w2, gate, offs, out):
                 d[name] = g
             return d[name]
 
-        def plain(eng, g, raw, lo, hi):
-            COPY[eng](
-                g[:, lo:hi, :].rearrange("p (c i) j -> p c j i", i=4),
-                raw[:, :, lo:hi].rearrange("p j (c i) -> p c j i", i=4),
-            )
-
         def permuted(eng, g, raw, lo, hi):
             COPY[eng](
                 g[:].rearrange("p (t m) j -> p m j t", t=J)[:, lo:hi],
@@ -191,45 +183,50 @@ def tile_routed_moe_kernel(tc, xT, w1, w3, w2, gate, offs, out):
         def flat(g):
             return g[:].rearrange("p n j -> p (n j)")
 
-        def x_il(s, eng, lo, hi):
-            plain(eng, grouped(f"xg{s}", XS[s]), d[f"x{s}"], lo, hi)
+        def x_il(i, eng, a, b):
+            u, lo, hi = XPC[i]
+            COPY[eng](
+                x_pairs[u][:, lo + a : lo + b, :].rearrange("p (c i) e -> p c e i", i=4),
+                d[f"x{i}"][:, :, a:b].rearrange("p e (c i) -> p c e i", i=4),
+            )
 
-        def x_q(s):
-            lo = sum(XS[:s])
-            cols = slice(lo, lo + XS[s])
-            nc.vector.quantize_mx(out=x_words[:, cols].bitcast(FP8X4), scales=x_bytes[:, cols], in_=flat(d[f"xg{s}"]))
-
-        def gather(kind, lo, hi):
-            o = offsets[:, lo // 16 : hi // 16]
-            if kind == "w":
-                nc.vector.tensor_copy(g_words[:, lo:hi], x_words[:].indirect(o))
-            else:
-                nc.vector.tensor_copy(g_bytes[:, lo:hi], x_bytes[:].indirect(o))
+        def gather(u, lo, hi):
+            nc.vector.tensor_copy(
+                flat(g_x).bitcast(U32).rearrange("p (n u) -> p n u", u=2)[:, lo:hi, u],
+                flat(x_pairs[u]).bitcast(U32).indirect(offsets[:, lo // 16 : hi // 16]),
+            )
 
         def w_il(w, e, eng, lo, hi):
             if w == "w2":
-                plain(eng, grouped(f"w2g{e}", N), d[f"w2r{e}"], lo, hi)
+                g = held.tile([P, 2, N, J], BF16, name=f"w2g{e}", align_bytes=64)
+                COPY[eng](
+                    g[:].rearrange("p e (c i) j -> p e c j i", i=4),
+                    d[f"w2r{e}"][:].rearrange("p e j (c i) -> p e c j i", i=4),
+                )
+                d[f"w2g{e}"] = g
             else:
                 permuted(eng, grouped(f"{w}g{e}", H), d[f"{w}r{e}"], lo, hi)
 
-        def quantise(name, g, width):
+        def quantise(name, in_, width):
             words = held.tile([P, width], U32, name=f"{name}_words", align_bytes=64)
             scales = held.tile([P, width], U8, name=f"{name}_bytes", align_bytes=64)
-            nc.vector.quantize_mx(out=words[:].bitcast(FP8X4), scales=scales[:], in_=flat(g))
+            nc.vector.quantize_mx(out=words[:].bitcast(FP8X4), scales=scales[:], in_=in_)
             d[name] = (words, scales)
 
         def first(k, e, hf):
             wq = d[("w1" if k == "a" else "w3") + f"q{e}"]
             bank = psum.tile([P, J, HALF], F32, name=k)
-            cols = slice(e * C + hf * HALF, e * C + (hf + 1) * HALF)
+            lo = max(a for a in XQ if a <= e * C)
+            xq = d[f"xq{lo}"]
+            cols = slice(e * C - lo + hf * HALF, e * C - lo + (hf + 1) * HALF)
             for t in range(J):
                 m = slice(t * P, (t + 1) * P)
                 nc.tensor.matmul_mx(
                     out=bank[:, t, :],
                     lhsT=wq[0][:, m].bitcast(FP8X4),
                     lhsT_scale=wq[1][:, m],
-                    rhs=g_words[:, cols].bitcast(FP8X4),
-                    rhs_scale=g_bytes[:, cols],
+                    rhs=xq[0][:, cols].bitcast(FP8X4),
+                    rhs_scale=xq[1][:, cols],
                     start=True,
                     stop=True,
                 )
@@ -249,13 +246,27 @@ def tile_routed_moe_kernel(tc, xT, w1, w3, w2, gate, offs, out):
                 MULT,
             )
 
+        def hidden_q(e, hf):
+            if f"hq{e}" not in d:
+                words = held.tile([P, C], U32, name=f"hq{e}_words", align_bytes=64)
+                scales = held.tile([P, C], U8, name=f"hq{e}_bytes", align_bytes=64)
+                d[f"hq{e}"] = (words, scales)
+            words, scales = d[f"hq{e}"]
+            cols = slice(hf * HALF, (hf + 1) * HALF)
+            nc.vector.quantize_mx(
+                out=words[:, cols].bitcast(FP8X4),
+                scales=scales[:, cols],
+                in_=flat(d[f"h{e}"])[:, hf * HALF * J : (hf + 1) * HALF * J],
+            )
+
         def second(e):
             y = psum_y.tile([P, C], F32, name="y")
-            hq, w2q = d[f"hq{e}"], d[f"w2q{e}"]
+            hq, w2q = d[f"hq{e}"], d[f"w2q{e // 2}"]
+            m = slice(e % 2 * N, (e % 2 + 1) * N)
             nc.tensor.matmul_mx(
                 out=y[:],
-                lhsT=w2q[0][:].bitcast(FP8X4),
-                lhsT_scale=w2q[1][:],
+                lhsT=w2q[0][:, m].bitcast(FP8X4),
+                lhsT_scale=w2q[1][:, m],
                 rhs=hq[0][:].bitcast(FP8X4),
                 rhs_scale=hq[1][:],
                 start=True,
@@ -283,15 +294,18 @@ def tile_routed_moe_kernel(tc, xT, w1, w3, w2, gate, offs, out):
             if k == "xi":
                 x_il(o[1], o[2], o[3], o[4])
             elif k == "xq":
-                x_q(o[1])
+                quantise(f"xq{o[1]}", flat(g_x)[:, o[1] * J : o[2] * J], o[2] - o[1])
             elif k == "g":
                 gather(o[1], o[2], o[3])
             elif k == "wi":
                 w_il(o[1], o[2], o[3], o[4], o[5])
             elif k == "wq":
-                quantise(f"{o[1]}q{o[2]}", d[f"{o[1]}g{o[2]}"], N if o[1] == "w2" else H)
+                g = d[f"{o[1]}g{o[2]}"]
+                quantise(f"{o[1]}q{o[2]}", g[:].rearrange("p e n j -> p (e n j)") if o[1] == "w2" else flat(g), 2 * N if o[1] == "w2" else H)
             elif k == "hq":
-                quantise(f"hq{o[1]}", d[f"h{o[1]}"], C)
+                quantise(f"hq{o[1]}", flat(d[f"h{o[1]}"]), C)
+            elif k == "hqh":
+                hidden_q(o[1], o[2])
             elif k == "first":
                 first(o[1], o[2], o[3])
             elif k == "sig":

@@ -22,93 +22,90 @@ HALF = 128
 SCATTER = 'd'
 XPC = [(0, 0, 768), (0, 768, 1536), (1, 0, 896), (1, 896, 1536)]
 XQ = [0, 512]
-LOADS = ['x0', 'x1', 'offs', 'x2', 'x3', 'w1r0', 'w3r0', 'w1r1', 'w3r1', 'w2r0', 'w1r2', 'w1r3', 'w3r2', 'gate0', 'w3r3', 'w2r1', 'gate1']
+LOADS = ['x0', 'x1', 'offs', 'x2', 'x3', 'w1r0', 'w3r0', 'w1r1', 'w3r1', 'w2r0', 'w1r3', 'w1r2', 'w3r2', 'gate0', 'gate1', 'w3r3', 'w2r1']
 ORDER = [
-    ('xi', 0, 'V', 0, 448),
-    ('xi', 0, 'S', 448, 768),
+    ('xi', 0, 'S', 704, 768),
+    ('xi', 0, 'V', 0, 704),
     ('xi', 1, 'S', 576, 768),
     ('xi', 1, 'V', 0, 576),
     ('g', 0, 0, 1024),
-    ('xi', 2, 'S', 128, 896),
-    ('xi', 2, 'V', 0, 128),
-    ('xi', 3, 'V', 0, 512),
-    ('xi', 3, 'S', 512, 640),
+    ('xi', 2, 'S', 0, 896),
+    ('xi', 3, 'V', 0, 448),
+    ('xi', 3, 'S', 448, 640),
     ('g', 1, 0, 512),
-    ('wi', 'w1', 0, 'S', 0, 128),
+    ('wi', 'w1', 0, 'S', 0, 4),
     ('g', 1, 512, 1024),
     ('xq', 0, 512),
+    ('wi', 'w3', 0, 'S', 0, 4),
     ('xq', 512, 1024),
-    ('wi', 'w3', 0, 'S', 32, 128),
     ('wq', 'w1', 0),
-    ('wi', 'w3', 0, 'V', 0, 32),
     ('first', 'a', 0, 0),
-    ('wi', 'w1', 1, 'S', 96, 128),
-    ('wi', 'w1', 1, 'V', 0, 96),
+    ('wi', 'w1', 1, 'V', 0, 2),
+    ('wi', 'w1', 1, 'V', 2, 4),
     ('first', 'a', 0, 1),
     ('sig', 0, 0),
     ('wq', 'w3', 0),
     ('sig', 0, 1),
     ('wq', 'w1', 1),
     ('first', 'b', 0, 0),
+    ('wi', 'w3', 1, 'S', 2, 4),
     ('first', 'b', 0, 1),
-    ('wi', 'w3', 1, 'V', 0, 56),
-    ('wi', 'w3', 1, 'S', 56, 128),
+    ('wi', 'w3', 1, 'V', 0, 2),
     ('first', 'a', 1, 0),
-    ('h', 0, 0),
-    ('first', 'a', 1, 1),
     ('h', 0, 1),
     ('wi', 'w2', 0, 'S', 0, 128),
+    ('first', 'a', 1, 1),
     ('wq', 'w3', 1),
-    ('hq', 0),
+    ('h', 0, 0),
     ('first', 'b', 1, 0),
     ('sig', 1, 0),
-    ('wi', 'w1', 2, 'V', 0, 64),
-    ('first', 'b', 1, 1),
-    ('sig', 1, 1),
     ('wq', 'w2', 0),
+    ('first', 'b', 1, 1),
+    ('wi', 'w1', 3, 'S', 2, 4),
+    ('wi', 'w1', 3, 'V', 0, 2),
     ('h', 1, 0),
-    ('y', 0),
-    ('wi', 'w1', 2, 'S', 64, 128),
-    ('h', 1, 1),
-    ('wi', 'w1', 3, 'V', 0, 64),
-    ('wi', 'w1', 3, 'S', 64, 128),
-    ('hq', 1),
-    ('wq', 'w1', 2),
-    ('y', 1),
-    ('yc', 0),
+    ('sig', 1, 1),
+    ('hq', 0),
     ('wq', 'w1', 3),
-    ('first', 'a', 2, 0),
-    ('wi', 'w3', 2, 'S', 40, 128),
-    ('first', 'a', 2, 1),
-    ('wi', 'w3', 2, 'V', 0, 40),
+    ('y', 0),
+    ('wi', 'w1', 2, 'S', 2, 4),
+    ('wi', 'w1', 2, 'V', 0, 2),
     ('first', 'a', 3, 0),
+    ('h', 1, 1),
+    ('yc', 0),
+    ('wq', 'w1', 2),
+    ('sig', 3, 0),
+    ('hq', 1),
+    ('first', 'a', 2, 0),
+    ('wi', 'w3', 2, 'S', 2, 4),
+    ('wi', 'w3', 2, 'V', 0, 2),
+    ('y', 1),
+    ('first', 'a', 2, 1),
     ('scat', 0),
     ('yc', 1),
     ('sig', 2, 0),
     ('wq', 'w3', 2),
-    ('wi', 'w3', 3, 'S', 40, 128),
+    ('sig', 2, 1),
     ('first', 'a', 3, 1),
-    ('wi', 'w3', 3, 'V', 0, 40),
-    ('first', 'b', 2, 0),
     ('scat', 1),
+    ('wi', 'w3', 3, 'S', 0, 4),
+    ('first', 'b', 2, 0),
     ('first', 'b', 2, 1),
+    ('h', 2, 0),
+    ('h', 2, 1),
     ('wi', 'w2', 1, 'S', 0, 128),
     ('wq', 'w3', 3),
-    ('sig', 2, 1),
-    ('h', 2, 0),
+    ('hq', 2),
+    ('sig', 3, 1),
     ('first', 'b', 3, 0),
     ('wq', 'w2', 1),
-    ('sig', 3, 1),
     ('first', 'b', 3, 1),
-    ('h', 2, 1),
-    ('sig', 3, 0),
-    ('h', 3, 1),
-    ('hq', 2),
     ('h', 3, 0),
     ('y', 2),
+    ('h', 3, 1),
     ('yc', 2),
-    ('hqh', 3, 1),
     ('hqh', 3, 0),
+    ('hqh', 3, 1),
     ('scat', 2),
     ('y', 3),
     ('yc', 3),
@@ -176,8 +173,8 @@ def tile_routed_moe_kernel(tc, xT, w1, w3, w2, gate, offs, out):
 
         def permuted(eng, g, raw, lo, hi):
             COPY[eng](
-                g[:].rearrange("p (t m) j -> p m j t", t=J)[:, lo:hi],
-                raw[:].rearrange("p j (m t) -> p m j t", t=J)[:, lo:hi],
+                g[:].rearrange("p (t m) j -> p m j t", t=J)[:, :, :, lo:hi],
+                raw[:].rearrange("p j (m t) -> p m j t", t=J)[:, :, :, lo:hi],
             )
 
         def flat(g):

@@ -20,23 +20,26 @@ SIGMOID = mybir.ActivationFunctionType.Sigmoid
 
 HALF = 128
 SCATTER = 'd'
-XPC = [(0, 0, 768), (0, 768, 1536), (1, 0, 896), (1, 896, 1536)]
+XPC = [(0, 0, 896), (0, 896, 1536), (1, 0, 1024), (1, 1024, 1536)]
 XQ = [0, 512]
-LOADS = ['x0', 'x1', 'offs', 'x2', 'x3', 'w1r0', 'w3r0', 'w1r1', 'w3r1', 'w2r0', 'w1r3', 'w1r2', 'w3r2', 'gate0', 'gate1', 'w3r3', 'w2r1']
+LOADS = ['x0', 'x1', 'offs', 'x2', 'x3', 'w1r0', 'w3r0', 'w1r1', 'w3r1', 'w2r0', 'w1r3', 'w1r2', 'w3r2', 'gate0', 'w3r3', 'gate1', 'w2r1']
 ORDER = [
-    ('xi', 0, 'S', 704, 768),
-    ('xi', 0, 'V', 0, 704),
-    ('xi', 1, 'S', 576, 768),
-    ('xi', 1, 'V', 0, 576),
+    ('xi', 0, 'V', 0, 384),
+    ('xi', 0, 'S', 384, 896),
+    ('xi', 1, 'V', 0, 384),
+    ('xi', 1, 'S', 384, 640),
     ('g', 0, 0, 1024),
-    ('xi', 2, 'S', 0, 896),
-    ('xi', 3, 'V', 0, 448),
-    ('xi', 3, 'S', 448, 640),
+    ('xi', 2, 'S', 256, 1024),
+    ('xi', 2, 'V', 0, 256),
+    ('xi', 3, 'V', 0, 320),
+    ('xi', 3, 'S', 320, 512),
     ('g', 1, 0, 512),
-    ('wi', 'w1', 0, 'S', 0, 4),
+    ('wi', 'w1', 0, 'S', 0, 2),
+    ('wi', 'w1', 0, 'S', 2, 4),
     ('g', 1, 512, 1024),
     ('xq', 0, 512),
-    ('wi', 'w3', 0, 'S', 0, 4),
+    ('wi', 'w3', 0, 'S', 0, 2),
+    ('wi', 'w3', 0, 'S', 2, 4),
     ('xq', 512, 1024),
     ('wq', 'w1', 0),
     ('first', 'a', 0, 0),
@@ -88,7 +91,8 @@ ORDER = [
     ('sig', 2, 1),
     ('first', 'a', 3, 1),
     ('scat', 1),
-    ('wi', 'w3', 3, 'S', 0, 4),
+    ('wi', 'w3', 3, 'S', 0, 2),
+    ('wi', 'w3', 3, 'S', 2, 4),
     ('first', 'b', 2, 0),
     ('first', 'b', 2, 1),
     ('h', 2, 0),

from contextlib import ExitStack

import concourse.mybir as mybir

K, T, E, C, H, N = 512, 1536, 4, 256, 512, 128
P = 128
J = 4
SLOTS = E * C
FLOPS = 2 * SLOTS * (2 * K * H + H * N)

F32 = mybir.dt.float32
BF16 = mybir.dt.bfloat16
U32 = mybir.dt.uint32
U16 = mybir.dt.uint16
U8 = mybir.dt.uint8
FP8X4 = mybir.dt.float8_e4m3fn_x4
MULT = mybir.AluOpType.mult
ADD = mybir.AluOpType.add
SIGMOID = mybir.ActivationFunctionType.Sigmoid

HALF = 128
SCATTER = 'd'
XPC = [(0, 0, 896), (0, 896, 1536), (1, 0, 1024), (1, 1024, 1536)]
XQ = [0, 512]
LOADS = ['x0', 'x1', 'offs', 'x2', 'x3', 'w1r0', 'w3r0', 'w1r1', 'w3r1', 'w2r0', 'w1r3', 'w1r2', 'w3r2', 'gate0', 'w3r3', 'gate1', 'w2r1']
ORDER = [
    ('xi', 0, 'V', 0, 384),
    ('xi', 0, 'S', 384, 896),
    ('xi', 1, 'V', 0, 384),
    ('xi', 1, 'S', 384, 640),
    ('g', 0, 0, 1024),
    ('xi', 2, 'S', 256, 1024),
    ('xi', 2, 'V', 0, 256),
    ('xi', 3, 'V', 0, 320),
    ('xi', 3, 'S', 320, 512),
    ('g', 1, 0, 512),
    ('wi', 'w1', 0, 'S', 0, 2),
    ('wi', 'w1', 0, 'S', 2, 4),
    ('g', 1, 512, 1024),
    ('xq', 0, 512),
    ('wi', 'w3', 0, 'S', 0, 2),
    ('wi', 'w3', 0, 'S', 2, 4),
    ('xq', 512, 1024),
    ('wq', 'w1', 0),
    ('first', 'a', 0, 0),
    ('wi', 'w1', 1, 'V', 0, 2),
    ('wi', 'w1', 1, 'V', 2, 4),
    ('first', 'a', 0, 1),
    ('sig', 0, 0),
    ('wq', 'w3', 0),
    ('sig', 0, 1),
    ('wq', 'w1', 1),
    ('first', 'b', 0, 0),
    ('wi', 'w3', 1, 'S', 2, 4),
    ('first', 'b', 0, 1),
    ('wi', 'w3', 1, 'V', 0, 2),
    ('first', 'a', 1, 0),
    ('h', 0, 1),
    ('wi', 'w2', 0, 'S', 0, 128),
    ('first', 'a', 1, 1),
    ('wq', 'w3', 1),
    ('h', 0, 0),
    ('first', 'b', 1, 0),
    ('sig', 1, 0),
    ('wq', 'w2', 0),
    ('first', 'b', 1, 1),
    ('wi', 'w1', 3, 'S', 2, 4),
    ('wi', 'w1', 3, 'V', 0, 2),
    ('h', 1, 0),
    ('sig', 1, 1),
    ('hq', 0),
    ('wq', 'w1', 3),
    ('y', 0),
    ('wi', 'w1', 2, 'S', 2, 4),
    ('wi', 'w1', 2, 'V', 0, 2),
    ('first', 'a', 3, 0),
    ('h', 1, 1),
    ('yc', 0),
    ('wq', 'w1', 2),
    ('sig', 3, 0),
    ('hq', 1),
    ('first', 'a', 2, 0),
    ('wi', 'w3', 2, 'S', 2, 4),
    ('wi', 'w3', 2, 'V', 0, 2),
    ('y', 1),
    ('first', 'a', 2, 1),
    ('scat', 0),
    ('yc', 1),
    ('sig', 2, 0),
    ('wq', 'w3', 2),
    ('sig', 2, 1),
    ('first', 'a', 3, 1),
    ('scat', 1),
    ('wi', 'w3', 3, 'S', 0, 2),
    ('wi', 'w3', 3, 'S', 2, 4),
    ('first', 'b', 2, 0),
    ('first', 'b', 2, 1),
    ('h', 2, 0),
    ('h', 2, 1),
    ('wi', 'w2', 1, 'S', 0, 128),
    ('wq', 'w3', 3),
    ('hq', 2),
    ('sig', 3, 1),
    ('first', 'b', 3, 0),
    ('wq', 'w2', 1),
    ('first', 'b', 3, 1),
    ('h', 3, 0),
    ('y', 2),
    ('h', 3, 1),
    ('yc', 2),
    ('hqh', 3, 0),
    ('hqh', 3, 1),
    ('scat', 2),
    ('y', 3),
    ('yc', 3),
    ('scat', 3),
]


def tile_routed_moe_kernel(tc, xT, w1, w3, w2, gate, offs, out):
    nc = tc.nc
    with ExitStack() as ctx:
        held = ctx.enter_context(tc.tile_pool(name="held", bufs=1))
        psum = ctx.enter_context(tc.psum_pool(name="psum", bufs=3))
        psum_y = ctx.enter_context(tc.psum_pool(name="psum_y", bufs=2))

        offsets = held.tile([P, SLOTS // 16], U16, name="offsets")
        x_view = xT.rearrange("(p u e) n -> u p e n", u=2, e=2)
        gate_sb = held.tile([P, SLOTS], F32, name="gate_sb")
        x_pairs = [held.tile([P, T, 2], BF16, name=f"x_pairs{u}", align_bytes=64) for u in range(2)]
        g_x = held.tile([P, SLOTS, J], BF16, name="g_x", align_bytes=64)
        window = held.tile([P, T], F32, name="window", align_bytes=64)
        d = {}
        WEIGHTS = {"w1": (w1, H), "w3": (w3, H)}

        def load(name):
            if name == "offs":
                nc.sync.dma_start(offsets[:], offs)
            elif name.startswith("gate"):
                cols = slice(int(name[4:]) * 2 * C, (int(name[4:]) + 1) * 2 * C)
                nc.sync.dma_start(gate_sb[:, cols], gate[:, cols])
            elif name.startswith("x"):
                u, lo, hi = XPC[int(name[1:])]
                t = held.tile([P, 2, hi - lo], F32, name=f"{name}_raw", align_bytes=64)
                nc.sync.dma_start(t[:], x_view[u][:, :, lo:hi])
                d[name] = t
            elif name.startswith("w2"):
                k = int(name[3:])
                t = held.tile([P, 2, J, N], F32, name=f"{name}_raw", align_bytes=64)
                nc.sync.dma_start(t[:], w2[2 * k : 2 * k + 2].rearrange("e (p j) n -> p e j n", j=J))
                d[name] = t
            else:
                src, width = WEIGHTS[name[0:2]]
                t = held.tile([P, J, width], F32, name=f"{name}_raw", align_bytes=64)
                nc.sync.dma_start(t[:], src[int(name[3:])].rearrange("(p j) n -> p j n", j=J))
                d[name] = t

        for name in LOADS:
            load(name)

        warm = held.tile([P, 1], F32, name="warm")
        nc.vector.memset(warm[:], 0.0)
        warm_out = held.tile([P, 1], F32, name="warm_out")
        nc.scalar.activation(warm_out[:], warm[:], SIGMOID)
        nc.vector.memset(window[:], 0.0)

        def gp_copy(out, in_):
            nc.gpsimd.tensor_scalar(out, in_, 1.0, 0.0, MULT, ADD)

        COPY = {"V": nc.vector.tensor_copy, "S": nc.scalar.copy, "G": gp_copy, "P": nc.gpsimd.tensor_copy}

        def grouped(name, width):
            if name not in d:
                g = held.tile([P, width, J], BF16, name=f"{name}_g", align_bytes=64)
                d[name] = g
            return d[name]

        def permuted(eng, g, raw, lo, hi):
            COPY[eng](
                g[:].rearrange("p (t m) j -> p m j t", t=J)[:, :, :, lo:hi],
                raw[:].rearrange("p j (m t) -> p m j t", t=J)[:, :, :, lo:hi],
            )

        def flat(g):
            return g[:].rearrange("p n j -> p (n j)")

        def x_il(i, eng, a, b):
            u, lo, hi = XPC[i]
            COPY[eng](
                x_pairs[u][:, lo + a : lo + b, :].rearrange("p (c i) e -> p c e i", i=4),
                d[f"x{i}"][:, :, a:b].rearrange("p e (c i) -> p c e i", i=4),
            )

        def gather(u, lo, hi):
            nc.vector.tensor_copy(
                flat(g_x).bitcast(U32).rearrange("p (n u) -> p n u", u=2)[:, lo:hi, u],
                flat(x_pairs[u]).bitcast(U32).indirect(offsets[:, lo // 16 : hi // 16]),
            )

        def w_il(w, e, eng, lo, hi):
            if w == "w2":
                g = held.tile([P, 2, N, J], BF16, name=f"w2g{e}", align_bytes=64)
                COPY[eng](
                    g[:].rearrange("p e (c i) j -> p e c j i", i=4),
                    d[f"w2r{e}"][:].rearrange("p e j (c i) -> p e c j i", i=4),
                )
                d[f"w2g{e}"] = g
            else:
                permuted(eng, grouped(f"{w}g{e}", H), d[f"{w}r{e}"], lo, hi)

        def quantise(name, in_, width):
            words = held.tile([P, width], U32, name=f"{name}_words", align_bytes=64)
            scales = held.tile([P, width], U8, name=f"{name}_bytes", align_bytes=64)
            nc.vector.quantize_mx(out=words[:].bitcast(FP8X4), scales=scales[:], in_=in_)
            d[name] = (words, scales)

        def first(k, e, hf):
            wq = d[("w1" if k == "a" else "w3") + f"q{e}"]
            bank = psum.tile([P, J, HALF], F32, name=k)
            lo = max(a for a in XQ if a <= e * C)
            xq = d[f"xq{lo}"]
            cols = slice(e * C - lo + hf * HALF, e * C - lo + (hf + 1) * HALF)
            for t in range(J):
                m = slice(t * P, (t + 1) * P)
                nc.tensor.matmul_mx(
                    out=bank[:, t, :],
                    lhsT=wq[0][:, m].bitcast(FP8X4),
                    lhsT_scale=wq[1][:, m],
                    rhs=xq[0][:, cols].bitcast(FP8X4),
                    rhs_scale=xq[1][:, cols],
                    start=True,
                    stop=True,
                )
            d[f"{k}{e}{hf}"] = bank

        def sig(e, hf):
            sg = held.tile([P, HALF, J], F32, name=f"sig{e}{hf}")
            nc.scalar.activation(sg[:], d[f"a{e}{hf}"][:].rearrange("p t c -> p c t"), SIGMOID)
            d[f"sig{e}{hf}"] = sg

        def hidden(e, hf):
            h = grouped(f"h{e}", C)
            nc.vector.tensor_tensor(
                h[:, hf * HALF : (hf + 1) * HALF, :],
                d[f"sig{e}{hf}"][:],
                d[f"b{e}{hf}"][:].rearrange("p t c -> p c t"),
                MULT,
            )

        def hidden_q(e, hf):
            if f"hq{e}" not in d:
                words = held.tile([P, C], U32, name=f"hq{e}_words", align_bytes=64)
                scales = held.tile([P, C], U8, name=f"hq{e}_bytes", align_bytes=64)
                d[f"hq{e}"] = (words, scales)
            words, scales = d[f"hq{e}"]
            cols = slice(hf * HALF, (hf + 1) * HALF)
            nc.vector.quantize_mx(
                out=words[:, cols].bitcast(FP8X4),
                scales=scales[:, cols],
                in_=flat(d[f"h{e}"])[:, hf * HALF * J : (hf + 1) * HALF * J],
            )

        def second(e):
            y = psum_y.tile([P, C], F32, name="y")
            hq, w2q = d[f"hq{e}"], d[f"w2q{e // 2}"]
            m = slice(e % 2 * N, (e % 2 + 1) * N)
            nc.tensor.matmul_mx(
                out=y[:],
                lhsT=w2q[0][:, m].bitcast(FP8X4),
                lhsT_scale=w2q[1][:, m],
                rhs=hq[0][:].bitcast(FP8X4),
                rhs_scale=hq[1][:],
                start=True,
                stop=True,
            )
            d[f"y{e}"] = y

        def y_copy(e):
            t = held.tile([P, C], F32, name=f"yc{e}")
            if SCATTER == "d":
                nc.scalar.copy(t[:], d[f"y{e}"][:])
            else:
                nc.vector.tensor_tensor(t[:], d[f"y{e}"][:], gate_sb[:, e * C : (e + 1) * C], MULT)
            d[f"yc{e}"] = t

        def scatter(e):
            w = window[:].indirect(offsets[:, e * (C // 16) : (e + 1) * (C // 16)])
            if SCATTER == "d":
                nc.vector.tensor_tensor(w, d[f"yc{e}"][:], gate_sb[:, e * C : (e + 1) * C], MULT)
            else:
                nc.vector.tensor_copy(w, d[f"yc{e}"][:])

        for o in ORDER:
            k = o[0]
            if k == "xi":
                x_il(o[1], o[2], o[3], o[4])
            elif k == "xq":
                quantise(f"xq{o[1]}", flat(g_x)[:, o[1] * J : o[2] * J], o[2] - o[1])
            elif k == "g":
                gather(o[1], o[2], o[3])
            elif k == "wi":
                w_il(o[1], o[2], o[3], o[4], o[5])
            elif k == "wq":
                g = d[f"{o[1]}g{o[2]}"]
                quantise(f"{o[1]}q{o[2]}", g[:].rearrange("p e n j -> p (e n j)") if o[1] == "w2" else flat(g), 2 * N if o[1] == "w2" else H)
            elif k == "hq":
                quantise(f"hq{o[1]}", flat(d[f"h{o[1]}"]), C)
            elif k == "hqh":
                hidden_q(o[1], o[2])
            elif k == "first":
                first(o[1], o[2], o[3])
            elif k == "sig":
                sig(o[1], o[2])
            elif k == "h":
                hidden(o[1], o[2])
            elif k == "y":
                second(o[1])
            elif k == "yc":
                y_copy(o[1])
            else:
                scatter(o[1])
        nc.sync.dma_start(out, window[:])
